import numpy as np
import ml_dtypes


def mxq(x, axis, fmt="e4m3"):
    dtype, down = {"e4m3": (ml_dtypes.float8_e4m3fn, 7), "e5m2": (ml_dtypes.float8_e5m2, 14)}[fmt]
    v = np.moveaxis(np.asarray(x, np.float32).astype(ml_dtypes.bfloat16).astype(np.float64), axis, -1)
    blocks = v.reshape(v.shape[:-1] + (-1, 32))
    amax = np.abs(blocks).max(-1, keepdims=True)
    byte = np.maximum(np.where(amax > 0, np.frexp(amax)[1] - 1 + 127, 0) - down, 1)
    scale = np.exp2(byte - 127.0)
    codes = (blocks / scale).astype(np.float32).astype(dtype).astype(np.float64)
    return np.moveaxis((codes * scale).reshape(v.shape), -1, axis)


WIDE = False


def mx_kscale(k, group=512):
    if not WIDE:
        return np.ones(k)
    levels = np.array([18, -18])
    if group != 512:
        return np.exp2(np.random.permutation(np.resize(levels, k // group))).repeat(group)
    if k % 512:
        return np.exp2(np.random.permutation(np.resize(levels, k // 32))).repeat(32)
    a = np.empty((k // 512, 16))
    for p in range(k // 512):
        a[p, :8] = np.random.permutation(np.resize(levels, 8))
        for g in range(8):
            far = levels[np.abs(levels - a[p, g]) >= 10]
            a[p, g + 8] = far[np.random.randint(len(far))]
    return np.exp2(a.ravel()).repeat(32)


def f64(x):
    return np.asarray(x).astype(np.float64)


G, D, M, N = 4, 128, 128, 1024


def setup_inputs():
    n = np.random.standard_normal
    s = mx_kscale(D, 0)[:, None]
    return {
        "x": (n((G, D, N)) * s).astype(np.float32),
        "w": (n((G, D, M)) / np.sqrt(D) / s).astype(np.float32),
        "b": (0.5 * n((G, M, 1))).astype(np.float32),
        "r": n((G, M, N)).astype(np.float32),
    }


def reference(x, w, b, r):
    xq = mxq(f64(x), 1, "e4m3")
    y = mxq(f64(w), 1, "e4m3").transpose(0, 2, 1) @ xq
    y = y + f64(b)
    y = y + f64(r)
    return y

@@ -1,0 +1,103 @@
+from contextlib import ExitStack
+
+import concourse.mybir as mybir
+
+G, D, M, N = 4, 128, 128, 1024
+FLOPS = 2 * G * D * M * N
+
+F32 = mybir.dt.float32
+BF16 = mybir.dt.bfloat16
+U32 = mybir.dt.uint32
+U8 = mybir.dt.uint8
+FP8X4 = mybir.dt.float8_e4m3fn_x4
+ADD = mybir.AluOpType.add
+
+P = 128
+PACK = 4
+ROWS = D // PACK
+HALF = 512
+VECTOR_COLS = 320
+
+
+def tile_rows_glin_bias_res_kernel(tc, x, w, b, r, out):
+    nc = tc.nc
+    halves = N // HALF
+    x_rows = x.rearrange("g (p j) n -> (g p) j n", j=PACK)
+    w_rows = w.rearrange("g (p j) m -> (g p) j m", j=PACK)
+
+    with ExitStack() as ctx:
+        sb = ctx.enter_context(tc.tile_pool(name="sb", bufs=1))
+        psum = ctx.enter_context(tc.psum_pool(name="psum", bufs=1))
+        ctx.enter_context(tc.manual_schedule())
+
+        x_raw = [sb.tile([P, PACK, HALF], F32, name="x_raw%d" % h) for h in range(halves)]
+        w_raw = sb.tile([P, PACK, M], F32, name="w_raw")
+        res = [sb.tile([P, N], F32, name="res%d" % g) for g in range(G)]
+        y = [sb.tile([P, N], F32, name="y%d" % g) for g in range(G)]
+        bias_rows = sb.tile([P, P], F32, name="bias_rows", align_bytes=64)
+        bias_cols = sb.tile([P, P], F32, name="bias_cols", align_bytes=64)
+        x_bf = [sb.tile([P, HALF, PACK], BF16, name="x_bf%d" % h, align_bytes=64) for h in range(halves)]
+        x_codes = [sb.tile([P, HALF], U32, name="x_codes%d" % h, align_bytes=64) for h in range(halves)]
+        x_scales = [sb.tile([P, HALF], U8, name="x_scales%d" % h, align_bytes=64) for h in range(halves)]
+        w_bf = sb.tile([P, M, PACK], BF16, name="w_bf", align_bytes=64)
+        w_codes = sb.tile([P, M], U32, name="w_codes", align_bytes=64)
+        w_scales = sb.tile([P, M], U8, name="w_scales", align_bytes=64)
+        acc = [[psum.tile([M, HALF], F32, name="acc%d_%d" % (h, g)) for g in range(G)] for h in range(halves)]
+
+        nc.vector.memset(bias_rows[:], 0.0)
+        nc.sync.dma_start(out=x_raw[0][:], in_=x_rows[:, :, 0:HALF])
+        nc.sync.dma_start(out=w_raw[:], in_=w_rows)
+        nc.scalar.dma_start(
+            out=bias_rows[0:P:32, :].rearrange("q (g i) -> q g i", g=G),
+            in_=b.rearrange("g (q i) o -> q g (i o)", i=32),
+        )
+        nc.sync.dma_start(out=x_raw[1][:], in_=x_rows[:, :, HALF:N])
+        for g in range(G):
+            nc.sync.dma_start(out=res[g][:], in_=r[g])
+
+        nc.vector.transpose(bias_cols[:], bias_rows[:])
+
+        def interleave_x(h):
+            src = x_raw[h][:].rearrange("p j n -> p n j")
+            nc.vector.tensor_copy(out=x_bf[h][:, 0:VECTOR_COLS, :], in_=src[:, 0:VECTOR_COLS, :])
+            nc.scalar.copy(out=x_bf[h][:, VECTOR_COLS:HALF, :], in_=src[:, VECTOR_COLS:HALF, :])
+
+        def quantize(codes, scales, grouped):
+            nc.vector.quantize_mx(
+                out=codes[:].bitcast(FP8X4), scales=scales[:], in_=grouped[:].rearrange("p c j -> p (c j)")
+            )
+
+        def multiply(h):
+            for g in range(G):
+                rows = slice(ROWS * g, ROWS * (g + 1))
+                nc.tensor.matmul_mx(
+                    out=acc[h][g][:],
+                    lhsT=w_codes[rows, :].bitcast(FP8X4),
+                    lhsT_scale=w_scales[rows, :],
+                    rhs=x_codes[h][rows, :].bitcast(FP8X4),
+                    rhs_scale=x_scales[h][rows, :],
+                    start=True,
+                    stop=True,
+                )
+
+        interleave_x(0)
+        nc.scalar.copy(out=w_bf[:], in_=w_raw[:].rearrange("p j m -> p m j"))
+        quantize(x_codes[0], x_scales[0], x_bf[0])
+        quantize(w_codes, w_scales, w_bf)
+        multiply(0)
+        interleave_x(1)
+        quantize(x_codes[1], x_scales[1], x_bf[1])
+        multiply(1)
+
+        for g in range(G):
+            for h in range(halves):
+                cols = slice(HALF * h, HALF * (h + 1))
+                nc.vector.scalar_tensor_tensor(
+                    out=y[g][:, cols],
+                    in0=acc[h][g][:],
+                    scalar=bias_cols[:, 32 * g : 32 * g + 1],
+                    in1=res[g][:, cols],
+                    op0=ADD,
+                    op1=ADD,
+                )
+            nc.sync.dma_start(out=out[g], in_=y[g][:])

@@ -47,15 +47,13 @@ def tile_rows_glin_bias_res_kernel(tc, x, w, b, r, out):
         nc.vector.memset(bias_rows[:], 0.0)
         nc.sync.dma_start(out=x_raw[0][:], in_=x_rows[:, :, 0:HALF])
         nc.sync.dma_start(out=w_raw[:], in_=w_rows)
-        nc.scalar.dma_start(
+        nc.sync.dma_start(
             out=bias_rows[0:P:32, :].rearrange("q (g i) -> q g i", g=G),
             in_=b.rearrange("g (q i) o -> q g (i o)", i=32),
         )
         nc.sync.dma_start(out=x_raw[1][:], in_=x_rows[:, :, HALF:N])
         for g in range(G):
             nc.sync.dma_start(out=res[g][:], in_=r[g])
-
-        nc.vector.transpose(bias_cols[:], bias_rows[:])
 
         def interleave_x(h):
             src = x_raw[h][:].rearrange("p j n -> p n j")
@@ -85,6 +83,7 @@ def tile_rows_glin_bias_res_kernel(tc, x, w, b, r, out):
         quantize(x_codes[0], x_scales[0], x_bf[0])
         quantize(w_codes, w_scales, w_bf)
         multiply(0)
+        nc.vector.transpose(bias_cols[:], bias_rows[:])
         interleave_x(1)
         quantize(x_codes[1], x_scales[1], x_bf[1])
         multiply(1)

@@ -16,7 +16,13 @@ P = 128
 PACK = 4
 ROWS = D // PACK
 HALF = 512
-VECTOR_COLS = 320
+QUARTER = 256
+EARLY = HALF + QUARTER
+LINE = 4
+SPLIT_HALF = 320
+SPLIT_THIRD = 128
+SPLIT_LAST = 160
+AHEAD = 2
 
 
 def tile_rows_glin_bias_res_kernel(tc, x, w, b, r, out):
@@ -30,13 +36,16 @@ def tile_rows_glin_bias_res_kernel(tc, x, w, b, r, out):
         psum = ctx.enter_context(tc.psum_pool(name="psum", bufs=1))
         ctx.enter_context(tc.manual_schedule())
 
-        x_raw = [sb.tile([P, PACK, HALF], F32, name="x_raw%d" % h) for h in range(halves)]
+        x_early = sb.tile([P, PACK, EARLY], F32, name="x_early")
+        x_late = sb.tile([P, PACK, QUARTER], F32, name="x_late")
         w_raw = sb.tile([P, PACK, M], F32, name="w_raw")
         res = [sb.tile([P, N], F32, name="res%d" % g) for g in range(G)]
         y = [sb.tile([P, N], F32, name="y%d" % g) for g in range(G)]
         bias_rows = sb.tile([P, P], F32, name="bias_rows", align_bytes=64)
         bias_cols = sb.tile([P, P], F32, name="bias_cols", align_bytes=64)
-        x_bf = [sb.tile([P, HALF, PACK], BF16, name="x_bf%d" % h, align_bytes=64) for h in range(halves)]
+        bf_half = sb.tile([P, HALF, PACK], BF16, name="bf_half", align_bytes=64)
+        bf_third = sb.tile([P, QUARTER, PACK], BF16, name="bf_third", align_bytes=64)
+        bf_last = sb.tile([P, QUARTER, PACK], BF16, name="bf_last", align_bytes=64)
         x_codes = [sb.tile([P, HALF], U32, name="x_codes%d" % h, align_bytes=64) for h in range(halves)]
         x_scales = [sb.tile([P, HALF], U8, name="x_scales%d" % h, align_bytes=64) for h in range(halves)]
         w_bf = sb.tile([P, M, PACK], BF16, name="w_bf", align_bytes=64)
@@ -45,48 +54,56 @@ def tile_rows_glin_bias_res_kernel(tc, x, w, b, r, out):
         acc = [[psum.tile([M, HALF], F32, name="acc%d_%d" % (h, g)) for g in range(G)] for h in range(halves)]
 
         nc.vector.memset(bias_rows[:], 0.0)
-        nc.sync.dma_start(out=x_raw[0][:], in_=x_rows[:, :, 0:HALF])
+        nc.sync.dma_start(out=x_early[:], in_=x_rows[:, :, 0:EARLY])
         nc.sync.dma_start(out=w_raw[:], in_=w_rows)
         nc.sync.dma_start(
             out=bias_rows[0:P:32, :].rearrange("q (g i) -> q g i", g=G),
             in_=b.rearrange("g (q i) o -> q g (i o)", i=32),
         )
-        nc.sync.dma_start(out=x_raw[1][:], in_=x_rows[:, :, HALF:N])
+        nc.sync.dma_start(out=x_late[:], in_=x_rows[:, :, EARLY:N])
         for g in range(G):
             nc.sync.dma_start(out=res[g][:], in_=r[g])
 
-        def interleave_x(h):
-            src = x_raw[h][:].rearrange("p j n -> p n j")
-            nc.vector.tensor_copy(out=x_bf[h][:, 0:VECTOR_COLS, :], in_=src[:, 0:VECTOR_COLS, :])
-            nc.scalar.copy(out=x_bf[h][:, VECTOR_COLS:HALF, :], in_=src[:, VECTOR_COLS:HALF, :])
-
-        def quantize(codes, scales, grouped):
-            nc.vector.quantize_mx(
-                out=codes[:].bitcast(FP8X4), scales=scales[:], in_=grouped[:].rearrange("p c j -> p (c j)")
+        def interleave(copy, grouped, raw):
+            copy(
+                out=grouped.rearrange("p (c i) j -> p c j i", i=LINE),
+                in_=raw.rearrange("p j (c i) -> p c j i", i=LINE),
             )
 
-        def multiply(h):
-            for g in range(G):
-                rows = slice(ROWS * g, ROWS * (g + 1))
-                nc.tensor.matmul_mx(
-                    out=acc[h][g][:],
-                    lhsT=w_codes[rows, :].bitcast(FP8X4),
-                    lhsT_scale=w_scales[rows, :],
-                    rhs=x_codes[h][rows, :].bitcast(FP8X4),
-                    rhs_scale=x_scales[h][rows, :],
-                    start=True,
-                    stop=True,
-                )
+        def quantize(codes, scales, grouped):
+            nc.vector.quantize_mx(out=codes.bitcast(FP8X4), scales=scales, in_=grouped.rearrange("p c j -> p (c j)"))
 
-        interleave_x(0)
-        nc.scalar.copy(out=w_bf[:], in_=w_raw[:].rearrange("p j m -> p m j"))
-        quantize(x_codes[0], x_scales[0], x_bf[0])
-        quantize(w_codes, w_scales, w_bf)
-        multiply(0)
+        def multiply(g, h):
+            rows = slice(ROWS * g, ROWS * (g + 1))
+            nc.tensor.matmul_mx(
+                out=acc[h][g][:],
+                lhsT=w_codes[rows, :].bitcast(FP8X4),
+                lhsT_scale=w_scales[rows, :],
+                rhs=x_codes[h][rows, :].bitcast(FP8X4),
+                rhs_scale=x_scales[h][rows, :],
+                start=True,
+                stop=True,
+            )
+
+        interleave(nc.scalar.copy, bf_half[:, SPLIT_HALF:HALF, :], x_early[:, :, SPLIT_HALF:HALF])
+        interleave(nc.scalar.copy, w_bf[:], w_raw[:])
+        interleave(nc.scalar.copy, bf_third[:, 0:SPLIT_THIRD, :], x_early[:, :, HALF : HALF + SPLIT_THIRD])
+        interleave(nc.scalar.copy, bf_last[:, SPLIT_LAST:QUARTER, :], x_late[:, :, SPLIT_LAST:QUARTER])
+
+        interleave(nc.vector.tensor_copy, bf_half[:, 0:SPLIT_HALF, :], x_early[:, :, 0:SPLIT_HALF])
+        interleave(nc.vector.tensor_copy, bf_third[:, SPLIT_THIRD:QUARTER, :], x_early[:, :, HALF + SPLIT_THIRD : EARLY])
+        quantize(x_codes[0][:], x_scales[0][:], bf_half[:])
+        quantize(w_codes[:], w_scales[:], w_bf[:])
+        for g in range(AHEAD):
+            multiply(g, 0)
         nc.vector.transpose(bias_cols[:], bias_rows[:])
-        interleave_x(1)
-        quantize(x_codes[1], x_scales[1], x_bf[1])
-        multiply(1)
+        interleave(nc.vector.tensor_copy, bf_last[:, 0:SPLIT_LAST, :], x_late[:, :, 0:SPLIT_LAST])
+        quantize(x_codes[1][:, 0:QUARTER], x_scales[1][:, 0:QUARTER], bf_third[:])
+        quantize(x_codes[1][:, QUARTER:HALF], x_scales[1][:, QUARTER:HALF], bf_last[:])
+        for g in range(G):
+            if g >= AHEAD:
+                multiply(g, 0)
+            multiply(g, 1)
 
         for g in range(G):
             for h in range(halves):

@@ -11,6 +11,7 @@ U32 = mybir.dt.uint32
 U8 = mybir.dt.uint8
 FP8X4 = mybir.dt.float8_e4m3fn_x4
 ADD = mybir.AluOpType.add
+IDENTITY = mybir.ActivationFunctionType.Identity
 
 P = 128
 PACK = 4
@@ -41,6 +42,7 @@ def tile_rows_glin_bias_res_kernel(tc, x, w, b, r, out):
         w_raw = sb.tile([P, PACK, M], F32, name="w_raw")
         res = [sb.tile([P, N], F32, name="res%d" % g) for g in range(G)]
         y = [sb.tile([P, N], F32, name="y%d" % g) for g in range(G)]
+        biased = sb.tile([P, HALF], F32, name="biased")
         bias_rows = sb.tile([P, P], F32, name="bias_rows", align_bytes=64)
         bias_cols = sb.tile([P, P], F32, name="bias_cols", align_bytes=64)
         bf_half = sb.tile([P, HALF, PACK], BF16, name="bf_half", align_bytes=64)
@@ -56,13 +58,15 @@ def tile_rows_glin_bias_res_kernel(tc, x, w, b, r, out):
         nc.vector.memset(bias_rows[:], 0.0)
         nc.sync.dma_start(out=x_early[:], in_=x_rows[:, :, 0:EARLY])
         nc.sync.dma_start(out=w_raw[:], in_=w_rows)
-        nc.sync.dma_start(
+        nc.scalar.dma_start(
             out=bias_rows[0:P:32, :].rearrange("q (g i) -> q g i", g=G),
             in_=b.rearrange("g (q i) o -> q g (i o)", i=32),
         )
         nc.sync.dma_start(out=x_late[:], in_=x_rows[:, :, EARLY:N])
         for g in range(G):
             nc.sync.dma_start(out=res[g][:], in_=r[g])
+
+        nc.vector.transpose(bias_cols[:], bias_rows[:])
 
         def interleave(copy, grouped, raw):
             copy(
@@ -96,7 +100,6 @@ def tile_rows_glin_bias_res_kernel(tc, x, w, b, r, out):
         quantize(w_codes[:], w_scales[:], w_bf[:])
         for g in range(AHEAD):
             multiply(g, 0)
-        nc.vector.transpose(bias_cols[:], bias_rows[:])
         interleave(nc.vector.tensor_copy, bf_last[:, 0:SPLIT_LAST, :], x_late[:, :, 0:SPLIT_LAST])
         quantize(x_codes[1][:, 0:QUARTER], x_scales[1][:, 0:QUARTER], bf_third[:])
         quantize(x_codes[1][:, QUARTER:HALF], x_scales[1][:, QUARTER:HALF], bf_last[:])
@@ -105,15 +108,28 @@ def tile_rows_glin_bias_res_kernel(tc, x, w, b, r, out):
                 multiply(g, 0)
             multiply(g, 1)
 
-        for g in range(G):
+        def add_on_vector(g, h):
+            cols = slice(HALF * h, HALF * (h + 1))
+            nc.vector.scalar_tensor_tensor(
+                out=y[g][:, cols],
+                in0=acc[h][g][:],
+                scalar=bias_cols[:, 32 * g : 32 * g + 1],
+                in1=res[g][:, cols],
+                op0=ADD,
+                op1=ADD,
+            )
+
+        for h in range(halves):
+            cols = slice(HALF * h, HALF * (h + 1))
+            add_on_vector(0, h)
+            nc.sync.dma_start(out=out[0][:, cols], in_=y[0][:, cols])
+
+        nc.scalar.activation(out=biased[:], in_=acc[0][1][:], func=IDENTITY, bias=bias_cols[:, 32:33])
+        nc.gpsimd.tensor_tensor(out=y[1][:, 0:HALF], in0=biased[:], in1=res[1][:, 0:HALF], op=ADD)
+        add_on_vector(1, 1)
+        nc.sync.dma_start(out=out[1], in_=y[1][:])
+
+        for g in range(2, G):
             for h in range(halves):
-                cols = slice(HALF * h, HALF * (h + 1))
-                nc.vector.scalar_tensor_tensor(
-                    out=y[g][:, cols],
-                    in0=acc[h][g][:],
-                    scalar=bias_cols[:, 32 * g : 32 * g + 1],
-                    in1=res[g][:, cols],
-                    op0=ADD,
-                    op1=ADD,
-                )
+                add_on_vector(g, h)
             nc.sync.dma_start(out=out[g], in_=y[g][:])

from contextlib import ExitStack

import concourse.mybir as mybir

G, D, M, N = 4, 128, 128, 1024
FLOPS = 2 * G * D * M * N

F32 = mybir.dt.float32
BF16 = mybir.dt.bfloat16
U32 = mybir.dt.uint32
U8 = mybir.dt.uint8
FP8X4 = mybir.dt.float8_e4m3fn_x4
ADD = mybir.AluOpType.add
IDENTITY = mybir.ActivationFunctionType.Identity

P = 128
PACK = 4
ROWS = D // PACK
HALF = 512
QUARTER = 256
EARLY = HALF + QUARTER
LINE = 4
SPLIT_HALF = 320
SPLIT_THIRD = 128
SPLIT_LAST = 160
AHEAD = 2


def tile_rows_glin_bias_res_kernel(tc, x, w, b, r, out):
    nc = tc.nc
    halves = N // HALF
    x_rows = x.rearrange("g (p j) n -> (g p) j n", j=PACK)
    w_rows = w.rearrange("g (p j) m -> (g p) j m", j=PACK)

    with ExitStack() as ctx:
        sb = ctx.enter_context(tc.tile_pool(name="sb", bufs=1))
        psum = ctx.enter_context(tc.psum_pool(name="psum", bufs=1))
        ctx.enter_context(tc.manual_schedule())

        x_early = sb.tile([P, PACK, EARLY], F32, name="x_early")
        x_late = sb.tile([P, PACK, QUARTER], F32, name="x_late")
        w_raw = sb.tile([P, PACK, M], F32, name="w_raw")
        res = [sb.tile([P, N], F32, name="res%d" % g) for g in range(G)]
        y = [sb.tile([P, N], F32, name="y%d" % g) for g in range(G)]
        biased = sb.tile([P, HALF], F32, name="biased")
        bias_rows = sb.tile([P, P], F32, name="bias_rows", align_bytes=64)
        bias_cols = sb.tile([P, P], F32, name="bias_cols", align_bytes=64)
        bf_half = sb.tile([P, HALF, PACK], BF16, name="bf_half", align_bytes=64)
        bf_third = sb.tile([P, QUARTER, PACK], BF16, name="bf_third", align_bytes=64)
        bf_last = sb.tile([P, QUARTER, PACK], BF16, name="bf_last", align_bytes=64)
        x_codes = [sb.tile([P, HALF], U32, name="x_codes%d" % h, align_bytes=64) for h in range(halves)]
        x_scales = [sb.tile([P, HALF], U8, name="x_scales%d" % h, align_bytes=64) for h in range(halves)]
        w_bf = sb.tile([P, M, PACK], BF16, name="w_bf", align_bytes=64)
        w_codes = sb.tile([P, M], U32, name="w_codes", align_bytes=64)
        w_scales = sb.tile([P, M], U8, name="w_scales", align_bytes=64)
        acc = [[psum.tile([M, HALF], F32, name="acc%d_%d" % (h, g)) for g in range(G)] for h in range(halves)]

        nc.vector.memset(bias_rows[:], 0.0)
        nc.sync.dma_start(out=x_early[:], in_=x_rows[:, :, 0:EARLY])
        nc.sync.dma_start(out=w_raw[:], in_=w_rows)
        nc.scalar.dma_start(
            out=bias_rows[0:P:32, :].rearrange("q (g i) -> q g i", g=G),
            in_=b.rearrange("g (q i) o -> q g (i o)", i=32),
        )
        nc.sync.dma_start(out=x_late[:], in_=x_rows[:, :, EARLY:N])
        for g in range(G):
            nc.sync.dma_start(out=res[g][:], in_=r[g])

        nc.vector.transpose(bias_cols[:], bias_rows[:])

        def interleave(copy, grouped, raw):
            copy(
                out=grouped.rearrange("p (c i) j -> p c j i", i=LINE),
                in_=raw.rearrange("p j (c i) -> p c j i", i=LINE),
            )

        def quantize(codes, scales, grouped):
            nc.vector.quantize_mx(out=codes.bitcast(FP8X4), scales=scales, in_=grouped.rearrange("p c j -> p (c j)"))

        def multiply(g, h):
            rows = slice(ROWS * g, ROWS * (g + 1))
            nc.tensor.matmul_mx(
                out=acc[h][g][:],
                lhsT=w_codes[rows, :].bitcast(FP8X4),
                lhsT_scale=w_scales[rows, :],
                rhs=x_codes[h][rows, :].bitcast(FP8X4),
                rhs_scale=x_scales[h][rows, :],
                start=True,
                stop=True,
            )

        interleave(nc.scalar.copy, bf_half[:, SPLIT_HALF:HALF, :], x_early[:, :, SPLIT_HALF:HALF])
        interleave(nc.scalar.copy, w_bf[:], w_raw[:])
        interleave(nc.scalar.copy, bf_third[:, 0:SPLIT_THIRD, :], x_early[:, :, HALF : HALF + SPLIT_THIRD])
        interleave(nc.scalar.copy, bf_last[:, SPLIT_LAST:QUARTER, :], x_late[:, :, SPLIT_LAST:QUARTER])

        interleave(nc.vector.tensor_copy, bf_half[:, 0:SPLIT_HALF, :], x_early[:, :, 0:SPLIT_HALF])
        interleave(nc.vector.tensor_copy, bf_third[:, SPLIT_THIRD:QUARTER, :], x_early[:, :, HALF + SPLIT_THIRD : EARLY])
        quantize(x_codes[0][:], x_scales[0][:], bf_half[:])
        quantize(w_codes[:], w_scales[:], w_bf[:])
        for g in range(AHEAD):
            multiply(g, 0)
        interleave(nc.vector.tensor_copy, bf_last[:, 0:SPLIT_LAST, :], x_late[:, :, 0:SPLIT_LAST])
        quantize(x_codes[1][:, 0:QUARTER], x_scales[1][:, 0:QUARTER], bf_third[:])
        quantize(x_codes[1][:, QUARTER:HALF], x_scales[1][:, QUARTER:HALF], bf_last[:])
        for g in range(G):
            if g >= AHEAD:
                multiply(g, 0)
            multiply(g, 1)

        def add_on_vector(g, h):
            cols = slice(HALF * h, HALF * (h + 1))
            nc.vector.scalar_tensor_tensor(
                out=y[g][:, cols],
                in0=acc[h][g][:],
                scalar=bias_cols[:, 32 * g : 32 * g + 1],
                in1=res[g][:, cols],
                op0=ADD,
                op1=ADD,
            )

        for h in range(halves):
            cols = slice(HALF * h, HALF * (h + 1))
            add_on_vector(0, h)
            nc.sync.dma_start(out=out[0][:, cols], in_=y[0][:, cols])

        nc.scalar.activation(out=biased[:], in_=acc[0][1][:], func=IDENTITY, bias=bias_cols[:, 32:33])
        nc.gpsimd.tensor_tensor(out=y[1][:, 0:HALF], in0=biased[:], in1=res[1][:, 0:HALF], op=ADD)
        add_on_vector(1, 1)
        nc.sync.dma_start(out=out[1], in_=y[1][:])

        for g in range(2, G):
            for h in range(halves):
                add_on_vector(g, h)
            nc.sync.dma_start(out=out[g], in_=y[g][:])
